import numpy as np, ml_dtypes
CORES = [37,45,53,61,69,109,117,125]
N = 8
import mx_ref
NC, NB = 128, 2
A = np.float32(0.0125)
SRC = [[(r - i) % N for i in range(NB)] for r in range(N)]
BF = ml_dtypes.bfloat16
def cut(t, i, w=512):
    return t[:, w * i:w * i + w]
def tile(rs):
    return np.stack(rs, axis=2).reshape(128, -1).astype(BF)
def setup_inputs(rng):
    def f(*shape):
        return mx_ref.flush((rng.standard_normal(shape, dtype=np.float32) * np.exp2(rng.integers(-2, 3, shape[:-1] + (1,)))).astype(BF))
    return {"q": f(N, 128, 4 * NC), "k": f(N, 128, 4 * 512), "v": f(N, 128, 512)}
def setup_inputs_blocks(rng):
    d = setup_inputs(rng)
    for k in ("v",): d[k] = mx_ref.spread(d[k], rng, 4)
    for k in ("q", "k"): d[k] = mx_ref.spread(d[k], rng, 1)
    return d
def setup_inputs_wide(rng):
    d = setup_inputs(rng)
    for k in ("v",): d[k] = mx_ref.flush((d[k].astype(np.float32) * np.exp2(rng.integers(-8, 9, (N, 1, 1))).astype(np.float32)).astype(BF))
    return d
def setup_inputs_sharp(rng):
    d = setup_inputs(rng); v = d["q"].astype(np.float32).reshape(N, 128, -1, 4)
    d["q"] = mx_ref.flush((v * np.exp2(rng.integers(-2, 4, (N, 1, v.shape[2], 1))).astype(np.float32)).reshape(d["q"].shape).astype(BF))
    return d
def setup_inputs_offset(rng):
    d = setup_inputs(rng); v = d["k"].astype(np.float32).reshape(N, 128, -1, 4)
    d["k"] = mx_ref.flush((v + 12 * rng.standard_normal((1, 128, 1, 4), dtype=np.float32)).reshape(d["k"].shape).astype(BF))
    return d
def reference(q, k, v, own=None):
    ONE = mx_ref.quantize(np.ones((128, 512), BF))
    K = [[mx_ref.quantize(cut(k[j], b)) for b in range(4)] for j in range(N)]; V = [mx_ref.quantize(v[j]) for j in range(N)]
    lo = np.zeros((N, NB, NC), np.float32); hi = lo.copy(); c = lo.copy(); w = lo.copy(); wlo = lo.copy(); whi = lo.copy(); p = np.zeros((N, NB, 128, 4 * NC), BF); o = np.zeros((N, 128, NC), np.float32)
    for r in range(N):
        Q = mx_ref.quantize(q[r])
        S = [[mx_ref.matmul(K[j][b], Q) * A for b in range(4)] for j in SRC[r]]
        lo[r] = [np.max(s, axis=(0, 1)) for s in S]; hi[r] = lo[r].max(axis=0) + 8
        c[r] = lo[r] if own is None else own["c"][r]
        for i in range(NB):
            p[r][i] = tile([np.exp(np.maximum(s - c[r][i], -20).astype(np.float64)).astype(np.float32) for s in S[i]])
        use = p[r] if own is None else own["p"][r]
        e = np.exp((c[r] - c[r].max(axis=0)).astype(np.float64)); wlo[r] = e * (1 - 4e-5); whi[r] = e * (1 + 4e-5)
        w[r] = e if own is None else own["w"][r]
        num = den = 0
        for i in range(NB):
            P = mx_ref.quantize(use[i])
            num = num + w[r][i].astype(np.float64) * mx_ref.matmul(V[SRC[r][i]], P); den = den + w[r][i].astype(np.float64) * mx_ref.matmul(ONE, P)
        o[r] = (num / den).astype(np.float32)
    return {"c": c, "c__lo": lo, "c__hi": hi, "p": p, "w": w, "w__lo": wlo, "w__hi": whi, "o": o}

import math
import numpy as np
from concourse.bass import DstId, RemoteDMATransfer
from concourse.mybir import dt, AluOpType, AxisListType, ActivationFunctionType

A32 = float(np.float32(0.0125))
FLOOR = math.exp(-20.0)
NCORES = 128
UNITS = 5

F, B, C8, U8 = "float32", "bfloat16", "float8_e4m3fn_x4", "uint8"
SCRATCH = {
    "kb": ("sbuf", [128, 2048], B), "vb": ("sbuf", [128, 512], B), "qb": ("sbuf", [128, 512], B),
    "oneb": ("sbuf", [128, 512], B),
    "kc": ("sbuf", [128, 512], C8), "kp": ("sbuf", [128, 512], U8),
    "vc": ("sbuf", [128, 128], C8), "vp": ("sbuf", [128, 128], U8),
    "qc": ("sbuf", [128, 128], C8), "qp": ("sbuf", [128, 128], U8),
    "onec": ("sbuf", [128, 128], C8), "onep": ("sbuf", [128, 128], U8),
    "rkc": ("sbuf", [128, 512], C8), "rkp": ("sbuf", [128, 512], U8),
    "rvc": ("sbuf", [128, 128], C8), "rvp": ("sbuf", [128, 128], U8),
    "ps": ("psum", [128, 4096], F),
    "pm": ("sbuf", [128, 8], F),
    "x0": ("sbuf", [128, 32], F), "x1": ("sbuf", [128, 32], F),
    "y0": ("sbuf", [128, 32], F), "y1": ("sbuf", [128, 32], F),
    "cb0": ("sbuf", [128, 128], F), "cb1": ("sbuf", [128, 128], F),
    "xs0": ("sbuf", [128, 512], F), "xs1": ("sbuf", [128, 512], F),
    "pt0": ("sbuf", [128, 512], B), "pt1": ("sbuf", [128, 512], B),
    "pc0": ("sbuf", [128, 128], C8), "pc1": ("sbuf", [128, 128], C8),
    "pp0": ("sbuf", [128, 128], U8), "pp1": ("sbuf", [128, 128], U8),
    "dd": ("sbuf", [128, 128], F), "w0b": ("sbuf", [128, 128], F), "wone": ("sbuf", [128, 128], F),
    "nl": ("sbuf", [128, 128], F), "na": ("sbuf", [128, 128], F), "den": ("sbuf", [128, 128], F),
    "rcp": ("sbuf", [128, 128], F), "num": ("sbuf", [128, 128], F), "ob": ("sbuf", [128, 128], F),
}
SEMAPHORES = (
    ["ld%d" % b for b in range(4)] + ["ldq", "ldv", "ms", "qzq", "qzo", "sent", "stored"]
    + ["qz%d" % u for u in range(UNITS)] + ["rc%d" % u for u in range(UNITS)]
    + ["rp%d" % u for u in range(UNITS)] + ["ar%d" % u for u in range(UNITS)]
    + ["st0", "rd0", "rn", "al0", "dds", "w0s", "nn", "l1", "a1", "dn", "rcs", "nm", "fo"]
    + ["t1_%d" % b for b in range(4)] + ["r1_%d" % b for b in range(4)]
    + ["%s%d" % (n, i) for n in ("cq", "tr", "xx", "cl", "qp") for i in range(2)]
    + ["%s%d_%d" % (n, i, a) for n in ("ss", "pb", "sb", "ex") for i in range(2) for a in range(4)]
)


def _bits(m):
    return bin(m).count("1")


def _helpers(src, dst, topo):
    cand = [c for c in range(NCORES) if c != src and topo.chip(c) == topo.chip(src) and topo.may_write(c, dst)]
    near = [c for c in cand if topo.die(c) == topo.die(src)]
    far = [c for c in cand if topo.die(c) != topo.die(src)]
    order = near[:1] + far[:1] + near[1:] + far[1:]
    return order[:2]


def _route(u):
    return 0 if u % 2 == 1 else 1


def _views(T, u, own):
    if u < 4:
        s = slice(128 * u, 128 * u + 128)
        return ((T.kc[:, s], T.kp[:, s]) if own else (T.rkc[:, s], T.rkp[:, s]))
    return ((T.vc[:], T.vp[:]) if own else (T.rvc[:], T.rvp[:]))


def _send(g, T, topo, src, dst, u, own, sem_codes, sem_plane, wait_codes=None, wait_plane=None):
    rid, pid, _ = topo.addr(dst)
    m = topo.mask(src, dst)
    sc, sp = _views(T, u, own)
    dc, dp = _views(T, u, False)
    if wait_codes is not None:
        g.wait_ge(wait_codes[0], wait_codes[1])
    g.remote_dma(out_ap=dc.bitcast(dt.uint8), in_ap=sc.bitcast(dt.uint8), remote_sem=sem_codes, local_sem=T.sem.sent,
                 pid=pid, routing_id=rid, dma_engine_mask=m)
    if wait_plane is not None:
        g.wait_ge(wait_plane[0], wait_plane[1])
    g.remote_dma(out_ap=dp, in_ap=sp, remote_sem=sem_plane, local_sem=T.sem.sent,
                 pid=pid, routing_id=rid, dma_engine_mask=m)
    return 2 * _bits(m)


def _helper_program(g, core, T, topo, src, dst, units):
    n = 0
    up = _bits(topo.mask(src, core))
    for u in units:
        ar = T.sem["ar%d" % u]
        n += _send(g, T, topo, core, dst, u, False, ar, ar, (T.sem["rc%d" % u], up), (T.sem["rp%d" % u], up))
    g.wait_ge(T.sem.sent, n)


def rank_program(g, core, T, topo):
    cores = list(T.cores)
    N = len(cores)
    rank = T.rank_of(core)
    if rank is None:
        for j in range(N):
            src, dst = cores[j], cores[(j + 1) % N]
            h = _helpers(src, dst, topo)
            if core in h:
                _helper_program(g, core, T, topo, src, dst, [u for u in range(UNITS) if h[_route(u)] == core])
        return

    V, S, TE, SY, sem = g.vector, g.scalar, g.tensor, g.sync, T.sem
    Alu, Act = AluOpType, ActivationFunctionType

    def bank(k, n=128):
        return T.ps[:, 512 * k:512 * k + n]

    for b in range(4):
        (SY if b % 2 == 0 else S).dma_start(T.kb[:, 512 * b:512 * b + 512], T.k[:, 512 * b:512 * b + 512]).then_inc(sem["ld%d" % b], 16)
    SY.dma_start(T.qb[:], T.q[:]).then_inc(sem.ldq, 16)
    S.dma_start(T.vb[:], T.v[:]).then_inc(sem.ldv, 16)

    V.memset(T.oneb[:], 1.0).then_inc(sem.ms, 1)
    V.memset(T.x0[:], 0.0).then_inc(sem.ms, 1)
    V.memset(T.x1[:], 0.0).then_inc(sem.ms, 1)
    V.memset(T.wone[0:1, :], 1.0).then_inc(sem.ms, 1)
    V.wait_ge(sem.ms, 4)
    V.quantize_mx(T.onec[:], T.onep[:], T.oneb[:]).then_inc(sem.qzo, 1)
    for b in range(4):
        s = slice(128 * b, 128 * b + 128)
        V.wait_ge(sem["ld%d" % b], 16)
        V.quantize_mx(T.kc[:, s], T.kp[:, s], T.kb[:, 512 * b:512 * b + 512]).then_inc(sem["qz%d" % b], 1)
    V.wait_ge(sem.ldq, 16)
    V.quantize_mx(T.qc[:], T.qp[:], T.qb[:]).then_inc(sem.qzq, 1)
    V.wait_ge(sem.ldv, 16)
    V.quantize_mx(T.vc[:], T.vp[:], T.vb[:]).then_inc(sem.qz4, 1)

    dst = cores[(rank + 1) % N]
    h = _helpers(core, dst, topo)
    nsent = 0
    for u in range(UNITS):
        g.wait_ge(sem["qz%d" % u], 1)
        nsent += _send(g, T, topo, core, h[_route(u)], u, True, sem["rc%d" % u], sem["rp%d" % u])

    prev = cores[(rank - 1) % N]
    hp = _helpers(prev, core, topo)
    landed = [2 * _bits(topo.mask(hp[_route(u)], core)) for u in range(UNITS)]

    TE.wait_ge(sem.qzq, 1)
    for b in range(4):
        TE.wait_ge(sem["qz%d" % b], 1)
    TE.matmul_mx(bank(4, 512), T.qc[:], T.qp[:], T.kc[:], T.kp[:], True, True).then_inc(sem.st0, 1)
    for b in range(4):
        s = slice(128 * b, 128 * b + 128)
        TE.matmul_mx(bank(b), T.kc[:, s], T.kp[:, s], T.qc[:], T.qp[:], True, True).then_inc(sem["ss0_%d" % b], 1)
    TE.wait_ge(sem.rd0, 1)
    TE.wait_ge(sem.xx0, 4)
    for b in range(4):
        s = slice(128 * b, 128 * b + 128)
        TE.wait_ge(sem["ar%d" % b], landed[b])
        if b >= 2:
            TE.wait_ge(sem["r1_%d" % (b - 2)], 1)
        TE.matmul_mx(bank(4 + b % 2), T.qc[:], T.qp[:], T.rkc[:, s], T.rkp[:, s], True, True).then_inc(sem["t1_%d" % b], 1)
        TE.matmul_mx(bank(b), T.rkc[:, s], T.rkp[:, s], T.qc[:], T.qp[:], True, True).then_inc(sem["ss1_%d" % b], 1)
    TE.wait_ge(sem.qp0, 1)
    TE.wait_ge(sem.qz4, 1)
    TE.wait_ge(sem.qzo, 1)
    TE.matmul_mx(bank(7), T.onec[:], T.onep[:], T.pc0[:], T.pp0[:], True, True).then_inc(sem.al0, 1)
    TE.matmul_mx(bank(6), T.vc[:], T.vp[:], T.pc0[:], T.pp0[:], True, True).then_inc(sem.al0, 1)
    TE.wait_ge(sem.qp1, 1)
    TE.wait_ge(sem.r1_2, 1)
    TE.wait_ge(sem.r1_3, 1)
    TE.matmul_mx(bank(5), T.onec[:], T.onep[:], T.pc1[:], T.pp1[:], True, True).then_inc(sem.l1, 1)
    TE.wait_ge(sem.ar4, landed[4])
    TE.matmul_mx(bank(4), T.rvc[:], T.rvp[:], T.pc1[:], T.pp1[:], True, True).then_inc(sem.a1, 1)

    def scale_scores(i):
        for b in range(4):
            S.wait_ge(sem["ss%d_%d" % (i, b)], 1)
            S.activation(out=T["xs%d" % i][:, b:512:4], in_=bank(b), func=Act.Copy, scale=A32).then_inc(sem["xx%d" % i], 1)

    def exps(i):
        for a in range(4):
            s = slice(128 * a, 128 * a + 128)
            S.wait_ge(sem["sb%d_%d" % (i, a)], 4)
            S.activation(out=T["pt%d" % i][:, s], in_=T["xs%d" % i][:, s], func=Act.Exp).then_inc(sem["ex%d_%d" % (i, a)], 1)

    scale_scores(0)
    exps(0)
    scale_scores(1)
    exps(1)
    S.wait_ge(sem.dds, 1)
    S.activation(out=T.w0b[:], in_=T.dd[:], func=Act.Exp).then_inc(sem.w0s, 1)

    def spread(i):
        g.wait_ge(sem["tr%d" % i], 1)
        for a in range(4):
            g.partition_broadcast(T["cb%d" % i][:, 32 * a:32 * a + 32], T["y%d" % i][32 * a:32 * a + 1, :], 128).then_inc(sem["pb%d_%d" % (i, a)], 1)

    spread(0)
    spread(1)
    g.wait_ge(sem.sent, nsent)

    def make_p(i, between=None):
        xs, pt, cb = T["xs%d" % i], T["pt%d" % i], T["cb%d" % i]
        V.wait_ge(sem["cq%d" % i], 1)
        V.transpose(T["y%d" % i][:], T["x%d" % i][:]).then_inc(sem["tr%d" % i], 1)
        V.wait_ge(sem["xx%d" % i], 4)

        def clamp(a):
            s = slice(128 * a, 128 * a + 128)
            V.wait_ge(sem["ex%d_%d" % (i, a)], 1)
            V.tensor_scalar(out=pt[:, s], in0=pt[:, s], scalar1=FLOOR, scalar2=None, op0=Alu.max).then_inc(sem["cl%d" % i], 1)

        for a in range(4):
            V.wait_ge(sem["pb%d_%d" % (i, a)], 1)
            for b in range(4):
                x = xs[:, 128 * a + b:128 * a + 128:4]
                V.tensor_tensor(out=x, in0=x, in1=cb[:, 32 * a:32 * a + 32], op=Alu.subtract).then_inc(sem["sb%d_%d" % (i, a)], 1)
            if a >= 1:
                clamp(a - 1)
        if between is not None:
            between()
        clamp(3)
        V.wait_ge(sem["cl%d" % i], 4)
        V.quantize_mx(T["pc%d" % i][:], T["pp%d" % i][:], pt[:]).then_inc(sem["qp%d" % i], 1)

    V.wait_ge(sem.st0, 1)
    V.tensor_reduce(out=T.pm[:, 0:1], in_=bank(4, 512), axis=AxisListType.X, op=Alu.max).then_inc(sem.rd0, 1)
    V.wait_ge(sem.rd0, 1)
    V.tensor_scalar(out=T.x0[:, 0:1], in0=T.pm[:, 0:1], scalar1=A32, scalar2=None, op0=Alu.mult).then_inc(sem.cq0, 1)
    make_p(0)
    for b in range(3):
        V.wait_ge(sem["t1_%d" % b], 1)
        V.tensor_reduce(out=T.pm[:, 1 + b:2 + b], in_=bank(4 + b % 2), axis=AxisListType.X, op=Alu.max).then_inc(sem["r1_%d" % b], 1)
    for b in range(3):
        V.wait_ge(sem["r1_%d" % b], 1)
    V.tensor_reduce(out=T.pm[:, 4:5], in_=T.pm[:, 0:4], axis=AxisListType.X, op=Alu.max).then_inc(sem.rn, 1)
    V.wait_ge(sem.t1_3, 1)
    V.tensor_reduce(out=T.pm[:, 5:6], in_=bank(5), axis=AxisListType.X, op=Alu.max).then_inc(sem.r1_3, 1)
    V.wait_ge(sem.r1_3, 1)
    V.wait_ge(sem.rn, 1)
    V.tensor_scalar(out=T.x1[:, 0:1], in0=T.pm[:, 5:6], scalar1=T.pm[:, 4:5], scalar2=A32, op0=Alu.max, op1=Alu.mult).then_inc(sem.cq1, 1)

    def shift_gap():
        V.tensor_tensor(out=T.dd[:], in0=T.cb0[:], in1=T.cb1[:], op=Alu.subtract).then_inc(sem.dds, 1)

    make_p(1, shift_gap)
    V.wait_ge(sem.w0s, 1)
    V.wait_ge(sem.al0, 2)
    V.tensor_tensor(out=T.nl[:], in0=bank(7), in1=T.w0b[:], op=Alu.mult).then_inc(sem.nn, 1)
    V.tensor_tensor(out=T.na[:], in0=bank(6), in1=T.w0b[:], op=Alu.mult).then_inc(sem.nn, 1)
    V.wait_ge(sem.nn, 2)
    V.wait_ge(sem.l1, 1)
    V.tensor_tensor(out=T.den[:], in0=bank(5), in1=T.nl[:], op=Alu.add).then_inc(sem.dn, 1)
    V.wait_ge(sem.dn, 1)
    V.reciprocal(out=T.rcp[:], in_=T.den[:]).then_inc(sem.rcs, 1)
    V.wait_ge(sem.a1, 1)
    V.tensor_tensor(out=T.num[:], in0=bank(4), in1=T.na[:], op=Alu.add).then_inc(sem.nm, 1)
    V.wait_ge(sem.rcs, 1)
    V.wait_ge(sem.nm, 1)
    V.tensor_tensor(out=T.ob[:], in0=T.num[:], in1=T.rcp[:], op=Alu.mult).then_inc(sem.fo, 1)

    SY.wait_ge(sem.ms, 4)
    SY.dma_start(T.w[1:2, :], T.wone[0:1, :]).then_inc(sem.stored, 16)
    for i in range(2):
        for a in range(4):
            SY.wait_ge(sem["pb%d_%d" % (i, a)], 1)
        SY.dma_start(T.c[i:i + 1, :], T["cb%d" % i][0:1, :]).then_inc(sem.stored, 16)
        SY.wait_ge(sem["cl%d" % i], 4)
        SY.dma_start(T.p[i], T["pt%d" % i][:]).then_inc(sem.stored, 16)
    SY.wait_ge(sem.w0s, 1)
    SY.dma_start(T.w[0:1, :], T.w0b[0:1, :]).then_inc(sem.stored, 16)
    SY.wait_ge(sem.fo, 1)
    SY.dma_start(T.o[:], T.ob[:]).then_inc(sem.stored, 16)
    SY.wait_ge(sem.stored, 16 * 7)
